import numpy as np
import ml_dtypes


def mxq(x, axis, fmt="e4m3"):
    dtype, down = {"e4m3": (ml_dtypes.float8_e4m3fn, 7), "e5m2": (ml_dtypes.float8_e5m2, 14)}[fmt]
    v = np.moveaxis(np.asarray(x, np.float32).astype(ml_dtypes.bfloat16).astype(np.float64), axis, -1)
    blocks = v.reshape(v.shape[:-1] + (-1, 32))
    amax = np.abs(blocks).max(-1, keepdims=True)
    byte = np.maximum(np.where(amax > 0, np.frexp(amax)[1] - 1 + 127, 0) - down, 1)
    scale = np.exp2(byte - 127.0)
    codes = (blocks / scale).astype(np.float32).astype(dtype).astype(np.float64)
    return np.moveaxis((codes * scale).reshape(v.shape), -1, axis)


WIDE = False


def mx_kscale(k):
    if not WIDE:
        return np.ones(k)
    levels = np.array([10, -10, 5, -5, 0])
    if k % 512:
        return np.exp2(np.random.permutation(np.resize(levels, k // 32))).repeat(32)
    a = np.empty((k // 512, 16))
    for p in range(k // 512):
        a[p, :8] = np.random.permutation(np.resize(levels, 8))
        for g in range(8):
            far = levels[np.abs(levels - a[p, g]) >= 10]
            a[p, g + 8] = far[np.random.randint(len(far))]
    return np.exp2(a.ravel()).repeat(32)


def f64(x):
    return np.asarray(x).astype(np.float64)


def striped8(idx):
    return np.concatenate([v.reshape(-1, 16).T for v in idx]).astype(np.uint16)


def unstriped8(offs):
    return np.stack([offs[16 * g:16 * g + 16].T.reshape(-1) for g in range(8)]).astype(np.int64)


def split(x):
    m, e = np.frexp(f64(x))
    hi = np.ldexp(np.trunc(16.0 * m) / 16.0, e)
    return hi, f64(x) - hi


K, M, T, S = 1024, 512, 2048, 1024


def setup_inputs():
    n = np.random.standard_normal
    s = mx_kscale(K)[:, None]
    return {
        "xT": (n((K, T)) * s).astype(np.float32),
        "w": (n((K, M)) / np.sqrt(K) / s).astype(np.float32),
        "wgt": np.repeat(np.random.uniform(0.5, 2.0, (8, S)), 16, axis=0).astype(np.float32),
        "b": (0.3 * n(512)).astype(np.float32),
        "offs": striped8(np.stack([np.random.permutation(T)[:S] for _ in range(8)])),
    }


def reference(xT, w, wgt, b, offs):
    idx = unstriped8(offs)
    group = np.arange(K) % 512 // 64
    xg = f64(wgt)[np.arange(K) // 4 % 128] * f64(xT)[np.arange(K)[:, None], idx[group]]
    xT_ = mxq(xg, 0, "e4m3")
    w_hi, w_lo = split(w)
    w_hi_, w_lo_ = mxq(w_hi, 0, "e4m3"), mxq(w_lo, 0, "e4m3")
    y = xT_.T @ w_hi_ + xT_.T @ w_lo_
    return y + f64(b)[None, :]

@@ -1,0 +1,209 @@
+import concourse.mybir as mybir
+
+K, M, T, S = 1024, 512, 2048, 1024
+P = 128
+PACK = 4
+PASSES = K // (P * PACK)
+
+F32 = mybir.dt.float32
+BF16 = mybir.dt.bfloat16
+I32 = mybir.dt.int32
+U32 = mybir.dt.uint32
+U16 = mybir.dt.uint16
+U8 = mybir.dt.uint8
+FP8X4 = mybir.dt.float8_e4m3fn_x4
+ALU = mybir.AluOpType
+
+FLOPS = 2 * 2 * K * M * S
+HI_MASK = -0x000F0010
+
+
+def tile_list_heads_tm_hl_bias_kernel(tc, xT, w, wgt, b, offs, out):
+    nc = tc.nc
+    x_view = xT.rearrange("(a p i) t -> a i p t", a=PASSES, i=PACK)
+    w_view = w.rearrange("(a p i) n -> a p i n", a=PASSES, i=PACK)
+
+    with (
+        tc.tile_pool(name="lists", bufs=1) as lists,
+        tc.tile_pool(name="keep", bufs=1) as keep,
+        tc.psum_pool(name="psum", bufs=1) as psum,
+    ):
+        offsets = lists.tile([P, S // 16], U16, name="offsets")
+        wgt_sb = keep.tile([P, S], F32, name="wgt_sb")
+        bias = keep.tile([P, M], F32, name="bias")
+        planes = [[keep.tile([P, T], F32, name=f"plane{a}{i}") for i in range(PACK)] for a in range(PASSES)]
+        w_sb = [keep.tile([P, PACK, M], F32, name=f"w_sb{a}") for a in range(PASSES)]
+        w_raw = [keep.tile([P, M, PACK], BF16, name=f"w_raw{a}", align_bytes=64) for a in range(PASSES)]
+        parts = [keep.tile([P, 2, M, PACK], BF16, name=f"parts{a}", align_bytes=64) for a in range(PASSES)]
+        w_codes = [keep.tile([P, 2 * M], U32, name=f"w_codes{a}", align_bytes=64) for a in range(PASSES)]
+        w_scales = [keep.tile([P, 2 * M], U8, name=f"w_scales{a}", align_bytes=64) for a in range(PASSES)]
+        hi32 = keep.tile([P, PACK, 256], F32, name="hi32")
+        picked = [keep.tile([P, PACK, S], F32, name=f"picked{a}") for a in range(PASSES)]
+        x_bf = [keep.tile([P, S, PACK], BF16, name=f"x_bf{a}", align_bytes=64) for a in range(PASSES)]
+        x_codes = [keep.tile([P, S], U32, name=f"x_codes{a}", align_bytes=64) for a in range(PASSES)]
+        x_scales = [keep.tile([P, S], U8, name=f"x_scales{a}", align_bytes=64) for a in range(PASSES)]
+        acc = [psum.tile([P, M], F32, name=f"acc{j}") for j in range(S // P)]
+        result = [keep.tile([P, M], F32, name=f"result{j}") for j in range(S // P)]
+
+        def load_w(a, n0, n1):
+            nc.sync.dma_start(out=w_sb[a][:, :, n0:n1], in_=w_view[a][:, :, n0:n1])
+
+        def load_plane(a, i):
+            nc.sync.dma_start(out=planes[a][i][:], in_=x_view[a, i])
+
+        def raw_w(a, n0, n1):
+            upper = w_sb[a][:].bitcast(BF16).rearrange("p i (n h) -> p i n h", h=2)[:, :, n0:n1, 1]
+            nc.scalar.copy(
+                out=w_raw[a][:, n0:n1, :].rearrange("p (c e) i -> p c i e", e=4),
+                in_=upper.rearrange("p i (c e) -> p c i e", e=4),
+            )
+
+        def mask_w(a, n0, n1):
+            nc.vector.tensor_scalar(
+                out=parts[a][:, 0, n0:n1, :].rearrange("p n i -> p (n i)").bitcast(I32),
+                in0=w_raw[a][:, n0:n1, :].rearrange("p n i -> p (n i)").bitcast(I32),
+                scalar1=HI_MASK,
+                scalar2=None,
+                op0=ALU.bitwise_and,
+            )
+
+        def rest_w(a, n0, n1):
+            nc.vector.tensor_tensor(
+                out=parts[a][:, 1, n0:n1, :],
+                in0=w_sb[a][:, :, n0:n1].rearrange("p i n -> p n i"),
+                in1=parts[a][:, 0, n0:n1, :],
+                op=ALU.subtract,
+            )
+
+        def mask_first(n0, n1):
+            nc.vector.tensor_scalar(
+                out=hi32[:, :, n0:n1].bitcast(I32),
+                in0=w_sb[0][:, :, n0:n1].bitcast(I32),
+                scalar1=-0x00100000,
+                scalar2=None,
+                op0=ALU.bitwise_and,
+            )
+            nc.scalar.copy(
+                out=parts[0][:, 0, n0:n1, :].rearrange("p (c e) i -> p c i e", e=4),
+                in_=hi32[:, :, n0:n1].rearrange("p i (c e) -> p c i e", e=4),
+            )
+
+        def rest_first(n0, n1):
+            nc.vector.tensor_tensor(
+                out=parts[0][:, 1, n0:n1, :],
+                in0=w_sb[0][:, :, n0:n1].rearrange("p i n -> p n i"),
+                in1=hi32[:, :, n0:n1].rearrange("p i n -> p n i"),
+                op=ALU.subtract,
+            )
+
+        def quantize_w(a, h):
+            nc.vector.quantize_mx(
+                out=w_codes[a][:, h * M : (h + 1) * M].bitcast(FP8X4),
+                scales=w_scales[a][:, h * M : (h + 1) * M],
+                in_=parts[a][:, h, :, :].rearrange("p n i -> p (n i)"),
+            )
+
+        def gather(a, i, j0, c):
+            nc.vector.tensor_tensor(
+                out=picked[a][:, i, j0 : j0 + c],
+                in0=planes[a][i][:].indirect(offsets[:, j0 // 16 : (j0 + c) // 16]),
+                in1=wgt_sb[:, j0 : j0 + c],
+                op=ALU.mult,
+            )
+
+        def interleave_x(a, j0, c):
+            nc.scalar.copy(
+                out=x_bf[a][:, j0 : j0 + c, :].rearrange("p (c e) i -> p c i e", e=4),
+                in_=picked[a][:, :, j0 : j0 + c].rearrange("p i (c e) -> p c i e", e=4),
+            )
+
+        def quantize_x(a, j0, c):
+            nc.vector.quantize_mx(
+                out=x_codes[a][:, j0 : j0 + c].bitcast(FP8X4),
+                scales=x_scales[a][:, j0 : j0 + c],
+                in_=x_bf[a][:, j0 : j0 + c, :].rearrange("p j i -> p (j i)"),
+            )
+
+        def multiply(a, j0, c):
+            for j in range(j0 // P, (j0 + c) // P):
+                cols = slice(j * P, (j + 1) * P)
+                for k in range(2):
+                    w_cols = slice(k * M, (k + 1) * M)
+                    nc.tensor.matmul_mx(
+                        out=acc[j][:],
+                        lhsT=x_codes[a][:, cols].bitcast(FP8X4),
+                        lhsT_scale=x_scales[a][:, cols],
+                        rhs=w_codes[a][:, w_cols].bitcast(FP8X4),
+                        rhs_scale=w_scales[a][:, w_cols],
+                        start=(a == 0 and k == 0),
+                        stop=(a == PASSES - 1 and k == 1),
+                    )
+
+        def finish(j0, c):
+            for j in range(j0 // P, (j0 + c) // P):
+                nc.vector.tensor_tensor(out=result[j][:], in0=acc[j][:], in1=bias[:], op=ALU.add)
+                nc.sync.dma_start(out=out[j * P : (j + 1) * P, :], in_=result[j][:])
+
+        load_w(0, 0, 256)
+        load_w(0, 256, 512)
+        nc.sync.dma_start(offsets[:], offs)
+        nc.sync.dma_start(out=wgt_sb[:], in_=wgt)
+        for i in range(PACK):
+            load_plane(0, i)
+        load_w(1, 0, 512)
+        for i in range(PACK):
+            load_plane(1, i)
+        nc.sync.dma_start(out=bias[:], in_=b.partition_broadcast(P))
+
+        mask_first(0, 128)
+        mask_first(128, 256)
+        raw_w(0, 256, 512)
+        rest_first(0, 128)
+        rest_first(128, 256)
+        mask_w(0, 256, 512)
+        quantize_w(0, 0)
+        rest_w(0, 256, 512)
+        gather(0, 0, 0, 512)
+        quantize_w(0, 1)
+        gather(0, 0, 512, 512)
+        for i in range(1, PACK - 1):
+            gather(0, i, 0, 512)
+            gather(0, i, 512, 512)
+        raw_w(1, 0, 512)
+        gather(0, 3, 0, 512)
+        interleave_x(0, 0, 512)
+        mask_w(1, 0, 512)
+        gather(0, 3, 512, 512)
+        interleave_x(0, 512, 512)
+        rest_w(1, 0, 512)
+        quantize_w(1, 0)
+        quantize_x(0, 0, 512)
+        quantize_w(1, 1)
+        multiply(0, 0, 512)
+        gather(1, 0, 0, 512)
+        quantize_x(0, 512, 512)
+        multiply(0, 512, 512)
+        for i in range(1, PACK):
+            gather(1, i, 0, 512)
+        interleave_x(1, 0, 512)
+        for i in range(PACK - 1):
+            gather(1, i, 512, 384)
+        quantize_x(1, 0, 512)
+        gather(1, 3, 512, 384)
+        interleave_x(1, 512, 256)
+        interleave_x(1, 768, 128)
+        multiply(1, 0, 512)
+        gather(1, 0, 896, 128)
+        gather(1, 1, 896, 128)
+        quantize_x(1, 512, 256)
+        gather(1, 2, 896, 128)
+        gather(1, 3, 896, 128)
+        interleave_x(1, 896, 128)
+        quantize_x(1, 768, 128)
+        finish(0, 256)
+        multiply(1, 512, 384)
+        quantize_x(1, 896, 128)
+        finish(256, 256)
+        multiply(1, 896, 128)
+        finish(512, 384)
+        finish(896, 128)

@@ -69,9 +69,9 @@ def tile_list_heads_tm_hl_bias_kernel(tc, xT, w, wgt, b, offs, out):
 
         def rest_w(a, n0, n1):
             nc.vector.tensor_tensor(
-                out=parts[a][:, 1, n0:n1, :],
-                in0=w_sb[a][:, :, n0:n1].rearrange("p i n -> p n i"),
-                in1=parts[a][:, 0, n0:n1, :],
+                out=parts[a][:, 1, n0:n1, :].rearrange("p (c e) i -> p c i e", e=4),
+                in0=w_sb[a][:, :, n0:n1].rearrange("p i (c e) -> p c i e", e=4),
+                in1=parts[a][:, 0, n0:n1, :].rearrange("p (c e) i -> p c i e", e=4),
                 op=ALU.subtract,
             )
 
@@ -90,9 +90,9 @@ def tile_list_heads_tm_hl_bias_kernel(tc, xT, w, wgt, b, offs, out):
 
         def rest_first(n0, n1):
             nc.vector.tensor_tensor(
-                out=parts[0][:, 1, n0:n1, :],
-                in0=w_sb[0][:, :, n0:n1].rearrange("p i n -> p n i"),
-                in1=hi32[:, :, n0:n1].rearrange("p i n -> p n i"),
+                out=parts[0][:, 1, n0:n1, :].rearrange("p (c e) i -> p c i e", e=4),
+                in0=w_sb[0][:, :, n0:n1].rearrange("p i (c e) -> p c i e", e=4),
+                in1=hi32[:, :, n0:n1].rearrange("p i (c e) -> p c i e", e=4),
                 op=ALU.subtract,
             )
 

@@ -33,11 +33,11 @@ def tile_list_heads_tm_hl_bias_kernel(tc, xT, w, wgt, b, offs, out):
         bias = keep.tile([P, M], F32, name="bias")
         planes = [[keep.tile([P, T], F32, name=f"plane{a}{i}") for i in range(PACK)] for a in range(PASSES)]
         w_sb = [keep.tile([P, PACK, M], F32, name=f"w_sb{a}") for a in range(PASSES)]
-        w_raw = [keep.tile([P, M, PACK], BF16, name=f"w_raw{a}", align_bytes=64) for a in range(PASSES)]
+        w_raw = keep.tile([P, M, PACK], BF16, name="w_raw", align_bytes=64)
         parts = [keep.tile([P, 2, M, PACK], BF16, name=f"parts{a}", align_bytes=64) for a in range(PASSES)]
         w_codes = [keep.tile([P, 2 * M], U32, name=f"w_codes{a}", align_bytes=64) for a in range(PASSES)]
         w_scales = [keep.tile([P, 2 * M], U8, name=f"w_scales{a}", align_bytes=64) for a in range(PASSES)]
-        hi32 = keep.tile([P, PACK, 256], F32, name="hi32")
+        hi32 = keep.tile([P, PACK, M], F32, name="hi32")
         picked = [keep.tile([P, PACK, S], F32, name=f"picked{a}") for a in range(PASSES)]
         x_bf = [keep.tile([P, S, PACK], BF16, name=f"x_bf{a}", align_bytes=64) for a in range(PASSES)]
         x_codes = [keep.tile([P, S], U32, name=f"x_codes{a}", align_bytes=64) for a in range(PASSES)]
@@ -45,54 +45,52 @@ def tile_list_heads_tm_hl_bias_kernel(tc, xT, w, wgt, b, offs, out):
         acc = [psum.tile([P, M], F32, name=f"acc{j}") for j in range(S // P)]
         result = [keep.tile([P, M], F32, name=f"result{j}") for j in range(S // P)]
 
-        def load_w(a, n0, n1):
-            nc.sync.dma_start(out=w_sb[a][:, :, n0:n1], in_=w_view[a][:, :, n0:n1])
+        def load_w(a, i0, i1):
+            nc.sync.dma_start(out=w_sb[a][:, i0:i1, :], in_=w_view[a][:, i0:i1, :])
 
         def load_plane(a, i):
             nc.sync.dma_start(out=planes[a][i][:], in_=x_view[a, i])
 
-        def raw_w(a, n0, n1):
-            upper = w_sb[a][:].bitcast(BF16).rearrange("p i (n h) -> p i n h", h=2)[:, :, n0:n1, 1]
+        def raw_w(n0, n1):
+            upper = w_sb[1][:].bitcast(BF16).rearrange("p i (n h) -> p i n h", h=2)[:, :, n0:n1, 1]
             nc.scalar.copy(
-                out=w_raw[a][:, n0:n1, :].rearrange("p (c e) i -> p c i e", e=4),
+                out=w_raw[:, n0:n1, :].rearrange("p (c e) i -> p c i e", e=4),
                 in_=upper.rearrange("p i (c e) -> p c i e", e=4),
             )
 
-        def mask_w(a, n0, n1):
+        def mask_packed(n0, n1):
             nc.vector.tensor_scalar(
-                out=parts[a][:, 0, n0:n1, :].rearrange("p n i -> p (n i)").bitcast(I32),
-                in0=w_raw[a][:, n0:n1, :].rearrange("p n i -> p (n i)").bitcast(I32),
+                out=parts[1][:, 0, n0:n1, :].rearrange("p n i -> p (n i)").bitcast(I32),
+                in0=w_raw[:, n0:n1, :].rearrange("p n i -> p (n i)").bitcast(I32),
                 scalar1=HI_MASK,
                 scalar2=None,
                 op0=ALU.bitwise_and,
             )
 
-        def rest_w(a, n0, n1):
-            nc.vector.tensor_tensor(
-                out=parts[a][:, 1, n0:n1, :].rearrange("p (c e) i -> p c i e", e=4),
-                in0=w_sb[a][:, :, n0:n1].rearrange("p i (c e) -> p c i e", e=4),
-                in1=parts[a][:, 0, n0:n1, :].rearrange("p (c e) i -> p c i e", e=4),
-                op=ALU.subtract,
-            )
-
-        def mask_first(n0, n1):
+        def mask_rows(i0, i1):
             nc.vector.tensor_scalar(
-                out=hi32[:, :, n0:n1].bitcast(I32),
-                in0=w_sb[0][:, :, n0:n1].bitcast(I32),
+                out=hi32[:, i0:i1, :].bitcast(I32),
+                in0=w_sb[0][:, i0:i1, :].bitcast(I32),
                 scalar1=-0x00100000,
                 scalar2=None,
                 op0=ALU.bitwise_and,
             )
+
+        def cast_hi():
             nc.scalar.copy(
-                out=parts[0][:, 0, n0:n1, :].rearrange("p (c e) i -> p c i e", e=4),
-                in_=hi32[:, :, n0:n1].rearrange("p i (c e) -> p c i e", e=4),
+                out=parts[0][:, 0, :, :].rearrange("p (c e) i -> p c i e", e=4),
+                in_=hi32[:].rearrange("p i (c e) -> p c i e", e=4),
             )
 
-        def rest_first(n0, n1):
+        def rest_w(a, n0, n1):
+            if a == 0:
+                hi = hi32[:, :, n0:n1].rearrange("p i (c e) -> p c i e", e=4)
+            else:
+                hi = parts[a][:, 0, n0:n1, :].rearrange("p (c e) i -> p c i e", e=4)
             nc.vector.tensor_tensor(
-                out=parts[0][:, 1, n0:n1, :].rearrange("p (c e) i -> p c i e", e=4),
-                in0=w_sb[0][:, :, n0:n1].rearrange("p i (c e) -> p c i e", e=4),
-                in1=hi32[:, :, n0:n1].rearrange("p i (c e) -> p c i e", e=4),
+                out=parts[a][:, 1, n0:n1, :].rearrange("p (c e) i -> p c i e", e=4),
+                in0=w_sb[a][:, :, n0:n1].rearrange("p i (c e) -> p c i e", e=4),
+                in1=hi,
                 op=ALU.subtract,
             )
 
@@ -144,66 +142,67 @@ def tile_list_heads_tm_hl_bias_kernel(tc, xT, w, wgt, b, offs, out):
                 nc.vector.tensor_tensor(out=result[j][:], in0=acc[j][:], in1=bias[:], op=ALU.add)
                 nc.sync.dma_start(out=out[j * P : (j + 1) * P, :], in_=result[j][:])
 
-        load_w(0, 0, 256)
-        load_w(0, 256, 512)
+        load_w(0, 0, 2)
+        load_w(0, 2, 4)
+        load_w(1, 0, 4)
         nc.sync.dma_start(offsets[:], offs)
         nc.sync.dma_start(out=wgt_sb[:], in_=wgt)
-        for i in range(PACK):
-            load_plane(0, i)
-        load_w(1, 0, 512)
-        for i in range(PACK):
-            load_plane(1, i)
+        for a, i in ((0, 0), (0, 1), (0, 2), (1, 0), (1, 1), (0, 3), (1, 2), (1, 3)):
+            load_plane(a, i)
         nc.sync.dma_start(out=bias[:], in_=b.partition_broadcast(P))
 
-        mask_first(0, 128)
-        mask_first(128, 256)
-        raw_w(0, 256, 512)
-        rest_first(0, 128)
-        rest_first(128, 256)
-        mask_w(0, 256, 512)
-        quantize_w(0, 0)
+        mask_rows(0, 2)
+        mask_rows(2, 4)
+        rest_w(0, 0, 256)
         rest_w(0, 256, 512)
-        gather(0, 0, 0, 512)
+        cast_hi()
+        raw_w(0, 256)
+        raw_w(256, 512)
+        mask_packed(0, 256)
         quantize_w(0, 1)
+        rest_w(1, 0, 256)
+        mask_packed(256, 512)
+        quantize_w(0, 0)
+        rest_w(1, 256, 512)
+        quantize_w(1, 0)
+        gather(0, 0, 0, 512)
+        quantize_w(1, 1)
         gather(0, 0, 512, 512)
         for i in range(1, PACK - 1):
             gather(0, i, 0, 512)
             gather(0, i, 512, 512)
-        raw_w(1, 0, 512)
+        gather(1, 0, 0, 640)
+        gather(1, 1, 0, 640)
         gather(0, 3, 0, 512)
         interleave_x(0, 0, 512)
-        mask_w(1, 0, 512)
         gather(0, 3, 512, 512)
         interleave_x(0, 512, 512)
-        rest_w(1, 0, 512)
-        quantize_w(1, 0)
+        gather(1, 2, 0, 640)
         quantize_x(0, 0, 512)
-        quantize_w(1, 1)
         multiply(0, 0, 512)
-        gather(1, 0, 0, 512)
+        gather(1, 3, 0, 640)
+        interleave_x(1, 0, 512)
+        interleave_x(1, 512, 128)
         quantize_x(0, 512, 512)
         multiply(0, 512, 512)
-        for i in range(1, PACK):
-            gather(1, i, 0, 512)
-        interleave_x(1, 0, 512)
-        for i in range(PACK - 1):
-            gather(1, i, 512, 384)
+        gather(1, 0, 640, 256)
+        gather(1, 1, 640, 256)
+        gather(1, 2, 640, 256)
         quantize_x(1, 0, 512)
-        gather(1, 3, 512, 384)
-        interleave_x(1, 512, 256)
-        interleave_x(1, 768, 128)
-        multiply(1, 0, 512)
+        gather(1, 3, 640, 256)
+        interleave_x(1, 640, 256)
+        quantize_x(1, 512, 128)
+        multiply(1, 0, 640)
         gather(1, 0, 896, 128)
         gather(1, 1, 896, 128)
-        quantize_x(1, 512, 256)
         gather(1, 2, 896, 128)
+        quantize_x(1, 640, 256)
         gather(1, 3, 896, 128)
         interleave_x(1, 896, 128)
-        quantize_x(1, 768, 128)
         finish(0, 256)
-        multiply(1, 512, 384)
+        multiply(1, 640, 256)
         quantize_x(1, 896, 128)
-        finish(256, 256)
+        finish(256, 384)
         multiply(1, 896, 128)
-        finish(512, 384)
+        finish(640, 256)
         finish(896, 128)

@@ -15,6 +15,8 @@ FP8X4 = mybir.dt.float8_e4m3fn_x4
 ALU = mybir.AluOpType
 
 FLOPS = 2 * 2 * K * M * S
+FIRST = 640
+PLANE_ORDER = ((0, 0), (0, 1), (0, 2), (1, 0), (1, 1), (0, 3), (1, 2), (1, 3))
 HI_MASK = -0x000F0010
 
 
@@ -30,6 +32,7 @@ def tile_list_heads_tm_hl_bias_kernel(tc, xT, w, wgt, b, offs, out):
     ):
         offsets = lists.tile([P, S // 16], U16, name="offsets")
         wgt_sb = keep.tile([P, S], F32, name="wgt_sb")
+        wgt_late = keep.tile([P, S - FIRST], F32, name="wgt_late")
         bias = keep.tile([P, M], F32, name="bias")
         planes = [[keep.tile([P, T], F32, name=f"plane{a}{i}") for i in range(PACK)] for a in range(PASSES)]
         w_sb = [keep.tile([P, PACK, M], F32, name=f"w_sb{a}") for a in range(PASSES)]
@@ -102,10 +105,12 @@ def tile_list_heads_tm_hl_bias_kernel(tc, xT, w, wgt, b, offs, out):
             )
 
         def gather(a, i, j0, c):
+            late = a == 1 and j0 >= FIRST
+            weights = wgt_late[:, j0 - FIRST : j0 - FIRST + c] if late else wgt_sb[:, j0 : j0 + c]
             nc.vector.tensor_tensor(
                 out=picked[a][:, i, j0 : j0 + c],
                 in0=planes[a][i][:].indirect(offsets[:, j0 // 16 : (j0 + c) // 16]),
-                in1=wgt_sb[:, j0 : j0 + c],
+                in1=weights,
                 op=ALU.mult,
             )
 
@@ -147,8 +152,9 @@ def tile_list_heads_tm_hl_bias_kernel(tc, xT, w, wgt, b, offs, out):
         load_w(1, 0, 4)
         nc.sync.dma_start(offsets[:], offs)
         nc.sync.dma_start(out=wgt_sb[:], in_=wgt)
-        for a, i in ((0, 0), (0, 1), (0, 2), (1, 0), (1, 1), (0, 3), (1, 2), (1, 3)):
+        for a, i in PLANE_ORDER:
             load_plane(a, i)
+        nc.sync.dma_start(out=wgt_late[:], in_=wgt[:, FIRST:S])
         nc.sync.dma_start(out=bias[:], in_=b.partition_broadcast(P))
 
         mask_rows(0, 2)
@@ -168,41 +174,34 @@ def tile_list_heads_tm_hl_bias_kernel(tc, xT, w, wgt, b, offs, out):
         gather(0, 0, 0, 512)
         quantize_w(1, 1)
         gather(0, 0, 512, 512)
-        for i in range(1, PACK - 1):
+        for i in (1, 2):
             gather(0, i, 0, 512)
             gather(0, i, 512, 512)
         gather(1, 0, 0, 640)
         gather(1, 1, 0, 640)
         gather(0, 3, 0, 512)
-        interleave_x(0, 0, 512)
+        interleave_x(0, 0, 256)
+        interleave_x(0, 256, 256)
         gather(0, 3, 512, 512)
-        interleave_x(0, 512, 512)
+        interleave_x(0, 512, 256)
+        interleave_x(0, 768, 256)
         gather(1, 2, 0, 640)
-        quantize_x(0, 0, 512)
-        multiply(0, 0, 512)
+        quantize_x(0, 0, 256)
+        multiply(0, 0, 256)
         gather(1, 3, 0, 640)
-        interleave_x(1, 0, 512)
-        interleave_x(1, 512, 128)
-        quantize_x(0, 512, 512)
-        multiply(0, 512, 512)
-        gather(1, 0, 640, 256)
-        gather(1, 1, 640, 256)
-        gather(1, 2, 640, 256)
-        quantize_x(1, 0, 512)
-        gather(1, 3, 640, 256)
+        for j0 in (256, 512, 768):
+            quantize_x(0, j0, 256)
+            multiply(0, j0, 256)
+        for j0, c in ((0, 256), (256, 256), (512, 128)):
+            interleave_x(1, j0, c)
+        for i in range(3):
+            gather(1, i, 640, 384)
+        quantize_x(1, 0, 256)
+        multiply(1, 0, 256)
+        gather(1, 3, 640, 384)
         interleave_x(1, 640, 256)
-        quantize_x(1, 512, 128)
-        multiply(1, 0, 640)
-        gather(1, 0, 896, 128)
-        gather(1, 1, 896, 128)
-        gather(1, 2, 896, 128)
-        quantize_x(1, 640, 256)
-        gather(1, 3, 896, 128)
         interleave_x(1, 896, 128)
-        finish(0, 256)
-        multiply(1, 640, 256)
-        quantize_x(1, 896, 128)
-        finish(256, 384)
-        multiply(1, 896, 128)
-        finish(640, 256)
-        finish(896, 128)
+        for j0, c in ((256, 256), (512, 128), (640, 256), (896, 128)):
+            quantize_x(1, j0, c)
+            multiply(1, j0, c)
+        finish(0, 1024)

import concourse.mybir as mybir

K, M, T, S = 1024, 512, 2048, 1024
P = 128
PACK = 4
PASSES = K // (P * PACK)

F32 = mybir.dt.float32
BF16 = mybir.dt.bfloat16
I32 = mybir.dt.int32
U32 = mybir.dt.uint32
U16 = mybir.dt.uint16
U8 = mybir.dt.uint8
FP8X4 = mybir.dt.float8_e4m3fn_x4
ALU = mybir.AluOpType

FLOPS = 2 * 2 * K * M * S
FIRST = 640
PLANE_ORDER = ((0, 0), (0, 1), (0, 2), (1, 0), (1, 1), (0, 3), (1, 2), (1, 3))
HI_MASK = -0x000F0010


def tile_list_heads_tm_hl_bias_kernel(tc, xT, w, wgt, b, offs, out):
    nc = tc.nc
    x_view = xT.rearrange("(a p i) t -> a i p t", a=PASSES, i=PACK)
    w_view = w.rearrange("(a p i) n -> a p i n", a=PASSES, i=PACK)

    with (
        tc.tile_pool(name="lists", bufs=1) as lists,
        tc.tile_pool(name="keep", bufs=1) as keep,
        tc.psum_pool(name="psum", bufs=1) as psum,
    ):
        offsets = lists.tile([P, S // 16], U16, name="offsets")
        wgt_sb = keep.tile([P, S], F32, name="wgt_sb")
        wgt_late = keep.tile([P, S - FIRST], F32, name="wgt_late")
        bias = keep.tile([P, M], F32, name="bias")
        planes = [[keep.tile([P, T], F32, name=f"plane{a}{i}") for i in range(PACK)] for a in range(PASSES)]
        w_sb = [keep.tile([P, PACK, M], F32, name=f"w_sb{a}") for a in range(PASSES)]
        w_raw = keep.tile([P, M, PACK], BF16, name="w_raw", align_bytes=64)
        parts = [keep.tile([P, 2, M, PACK], BF16, name=f"parts{a}", align_bytes=64) for a in range(PASSES)]
        w_codes = [keep.tile([P, 2 * M], U32, name=f"w_codes{a}", align_bytes=64) for a in range(PASSES)]
        w_scales = [keep.tile([P, 2 * M], U8, name=f"w_scales{a}", align_bytes=64) for a in range(PASSES)]
        hi32 = keep.tile([P, PACK, M], F32, name="hi32")
        picked = [keep.tile([P, PACK, S], F32, name=f"picked{a}") for a in range(PASSES)]
        x_bf = [keep.tile([P, S, PACK], BF16, name=f"x_bf{a}", align_bytes=64) for a in range(PASSES)]
        x_codes = [keep.tile([P, S], U32, name=f"x_codes{a}", align_bytes=64) for a in range(PASSES)]
        x_scales = [keep.tile([P, S], U8, name=f"x_scales{a}", align_bytes=64) for a in range(PASSES)]
        acc = [psum.tile([P, M], F32, name=f"acc{j}") for j in range(S // P)]
        result = [keep.tile([P, M], F32, name=f"result{j}") for j in range(S // P)]

        def load_w(a, i0, i1):
            nc.sync.dma_start(out=w_sb[a][:, i0:i1, :], in_=w_view[a][:, i0:i1, :])

        def load_plane(a, i):
            nc.sync.dma_start(out=planes[a][i][:], in_=x_view[a, i])

        def raw_w(n0, n1):
            upper = w_sb[1][:].bitcast(BF16).rearrange("p i (n h) -> p i n h", h=2)[:, :, n0:n1, 1]
            nc.scalar.copy(
                out=w_raw[:, n0:n1, :].rearrange("p (c e) i -> p c i e", e=4),
                in_=upper.rearrange("p i (c e) -> p c i e", e=4),
            )

        def mask_packed(n0, n1):
            nc.vector.tensor_scalar(
                out=parts[1][:, 0, n0:n1, :].rearrange("p n i -> p (n i)").bitcast(I32),
                in0=w_raw[:, n0:n1, :].rearrange("p n i -> p (n i)").bitcast(I32),
                scalar1=HI_MASK,
                scalar2=None,
                op0=ALU.bitwise_and,
            )

        def mask_rows(i0, i1):
            nc.vector.tensor_scalar(
                out=hi32[:, i0:i1, :].bitcast(I32),
                in0=w_sb[0][:, i0:i1, :].bitcast(I32),
                scalar1=-0x00100000,
                scalar2=None,
                op0=ALU.bitwise_and,
            )

        def cast_hi():
            nc.scalar.copy(
                out=parts[0][:, 0, :, :].rearrange("p (c e) i -> p c i e", e=4),
                in_=hi32[:].rearrange("p i (c e) -> p c i e", e=4),
            )

        def rest_w(a, n0, n1):
            if a == 0:
                hi = hi32[:, :, n0:n1].rearrange("p i (c e) -> p c i e", e=4)
            else:
                hi = parts[a][:, 0, n0:n1, :].rearrange("p (c e) i -> p c i e", e=4)
            nc.vector.tensor_tensor(
                out=parts[a][:, 1, n0:n1, :].rearrange("p (c e) i -> p c i e", e=4),
                in0=w_sb[a][:, :, n0:n1].rearrange("p i (c e) -> p c i e", e=4),
                in1=hi,
                op=ALU.subtract,
            )

        def quantize_w(a, h):
            nc.vector.quantize_mx(
                out=w_codes[a][:, h * M : (h + 1) * M].bitcast(FP8X4),
                scales=w_scales[a][:, h * M : (h + 1) * M],
                in_=parts[a][:, h, :, :].rearrange("p n i -> p (n i)"),
            )

        def gather(a, i, j0, c):
            late = a == 1 and j0 >= FIRST
            weights = wgt_late[:, j0 - FIRST : j0 - FIRST + c] if late else wgt_sb[:, j0 : j0 + c]
            nc.vector.tensor_tensor(
                out=picked[a][:, i, j0 : j0 + c],
                in0=planes[a][i][:].indirect(offsets[:, j0 // 16 : (j0 + c) // 16]),
                in1=weights,
                op=ALU.mult,
            )

        def interleave_x(a, j0, c):
            nc.scalar.copy(
                out=x_bf[a][:, j0 : j0 + c, :].rearrange("p (c e) i -> p c i e", e=4),
                in_=picked[a][:, :, j0 : j0 + c].rearrange("p i (c e) -> p c i e", e=4),
            )

        def quantize_x(a, j0, c):
            nc.vector.quantize_mx(
                out=x_codes[a][:, j0 : j0 + c].bitcast(FP8X4),
                scales=x_scales[a][:, j0 : j0 + c],
                in_=x_bf[a][:, j0 : j0 + c, :].rearrange("p j i -> p (j i)"),
            )

        def multiply(a, j0, c):
            for j in range(j0 // P, (j0 + c) // P):
                cols = slice(j * P, (j + 1) * P)
                for k in range(2):
                    w_cols = slice(k * M, (k + 1) * M)
                    nc.tensor.matmul_mx(
                        out=acc[j][:],
                        lhsT=x_codes[a][:, cols].bitcast(FP8X4),
                        lhsT_scale=x_scales[a][:, cols],
                        rhs=w_codes[a][:, w_cols].bitcast(FP8X4),
                        rhs_scale=w_scales[a][:, w_cols],
                        start=(a == 0 and k == 0),
                        stop=(a == PASSES - 1 and k == 1),
                    )

        def finish(j0, c):
            for j in range(j0 // P, (j0 + c) // P):
                nc.vector.tensor_tensor(out=result[j][:], in0=acc[j][:], in1=bias[:], op=ALU.add)
                nc.sync.dma_start(out=out[j * P : (j + 1) * P, :], in_=result[j][:])

        load_w(0, 0, 2)
        load_w(0, 2, 4)
        load_w(1, 0, 4)
        nc.sync.dma_start(offsets[:], offs)
        nc.sync.dma_start(out=wgt_sb[:], in_=wgt)
        for a, i in PLANE_ORDER:
            load_plane(a, i)
        nc.sync.dma_start(out=wgt_late[:], in_=wgt[:, FIRST:S])
        nc.sync.dma_start(out=bias[:], in_=b.partition_broadcast(P))

        mask_rows(0, 2)
        mask_rows(2, 4)
        rest_w(0, 0, 256)
        rest_w(0, 256, 512)
        cast_hi()
        raw_w(0, 256)
        raw_w(256, 512)
        mask_packed(0, 256)
        quantize_w(0, 1)
        rest_w(1, 0, 256)
        mask_packed(256, 512)
        quantize_w(0, 0)
        rest_w(1, 256, 512)
        quantize_w(1, 0)
        gather(0, 0, 0, 512)
        quantize_w(1, 1)
        gather(0, 0, 512, 512)
        for i in (1, 2):
            gather(0, i, 0, 512)
            gather(0, i, 512, 512)
        gather(1, 0, 0, 640)
        gather(1, 1, 0, 640)
        gather(0, 3, 0, 512)
        interleave_x(0, 0, 256)
        interleave_x(0, 256, 256)
        gather(0, 3, 512, 512)
        interleave_x(0, 512, 256)
        interleave_x(0, 768, 256)
        gather(1, 2, 0, 640)
        quantize_x(0, 0, 256)
        multiply(0, 0, 256)
        gather(1, 3, 0, 640)
        for j0 in (256, 512, 768):
            quantize_x(0, j0, 256)
            multiply(0, j0, 256)
        for j0, c in ((0, 256), (256, 256), (512, 128)):
            interleave_x(1, j0, c)
        for i in range(3):
            gather(1, i, 640, 384)
        quantize_x(1, 0, 256)
        multiply(1, 0, 256)
        gather(1, 3, 640, 384)
        interleave_x(1, 640, 256)
        interleave_x(1, 896, 128)
        for j0, c in ((256, 256), (512, 128), (640, 256), (896, 128)):
            quantize_x(1, j0, c)
            multiply(1, j0, c)
        finish(0, 1024)
